import numpy as np
import ml_dtypes


def mxq(x, axis, fmt="e4m3"):
    dtype, down = {"e4m3": (ml_dtypes.float8_e4m3fn, 7), "e5m2": (ml_dtypes.float8_e5m2, 14)}[fmt]
    v = np.moveaxis(np.asarray(x, np.float32).astype(ml_dtypes.bfloat16).astype(np.float64), axis, -1)
    blocks = v.reshape(v.shape[:-1] + (-1, 32))
    amax = np.abs(blocks).max(-1, keepdims=True)
    byte = np.maximum(np.where(amax > 0, np.frexp(amax)[1] - 1 + 127, 0) - down, 1)
    scale = np.exp2(byte - 127.0)
    codes = (blocks / scale).astype(np.float32).astype(dtype).astype(np.float64)
    return np.moveaxis((codes * scale).reshape(v.shape), -1, axis)


WIDE = False


def mx_kscale(k):
    if not WIDE:
        return np.ones(k)
    levels = np.array([10, -10, 5, -5, 0])
    if k % 512:
        return np.exp2(np.random.permutation(np.resize(levels, k // 32))).repeat(32)
    a = np.empty((k // 512, 16))
    for p in range(k // 512):
        a[p, :8] = np.random.permutation(np.resize(levels, 8))
        for g in range(8):
            far = levels[np.abs(levels - a[p, g]) >= 10]
            a[p, g + 8] = far[np.random.randint(len(far))]
    return np.exp2(a.ravel()).repeat(32)


def f64(x):
    return np.asarray(x).astype(np.float64)


def striped(idx):
    return np.tile(np.asarray(idx).reshape(-1, 16).T, (8, 1)).astype(np.uint16)


def unstriped(offs):
    return offs[:16].T.reshape(-1).astype(np.int64)


E2M1 = np.array([0.0, 0.5, 1.0, 1.5, 2.0, 3.0, 4.0, 6.0, -0.0, -0.5, -1.0, -1.5, -2.0, -3.0, -4.0, -6.0])


def pack_weight(w, fmt):
    k, n = w.shape
    w = f64(np.asarray(w, np.float32).astype(ml_dtypes.bfloat16)).reshape(k // 32, 32, n)
    amax = np.abs(w).max(1)
    if fmt == "e4m3":
        byte = np.frexp(amax)[1] - 1 + 127 - 7
    else:
        mant, ex = np.frexp(amax / 6.0)
        byte = np.where(mant > 0.5, ex, ex - 1) + 127
    byte = np.clip(np.where(amax > 0, byte, 1), 1, 254)
    scaled = (w * np.exp2(127.0 - byte)[:, None, :]).reshape(k, n).astype(np.float32)
    by_word = np.ascontiguousarray(scaled.reshape(k // 512, 128, 4, n).transpose(0, 1, 3, 2))
    if fmt == "e4m3":
        words = by_word.astype(ml_dtypes.float8_e4m3fn).view(np.uint8)
    else:
        c = by_word.astype(ml_dtypes.float4_e2m1fn).view(np.uint8) & 0xF
        words = (c[..., 0::2] | (c[..., 1::2] << 4)).reshape(k // 512, 128, 2 * n)
    return np.ascontiguousarray(words), np.ascontiguousarray(byte.astype(np.uint8).reshape(k // 512, 16, n))


def unpack_weight(words, scales, fmt):
    g, _, n = scales.shape
    words = np.ascontiguousarray(words).reshape(g, 128, n, -1)
    if fmt == "e4m3":
        vals = words.view(ml_dtypes.float8_e4m3fn).astype(np.float64)
    else:
        nib = np.empty((g, 128, n, 4), np.uint8)
        nib[..., 0::2] = words & 0xF
        nib[..., 1::2] = words >> 4
        vals = E2M1[nib]
    vals = vals * np.repeat(np.exp2(scales.astype(np.float64) - 127.0), 8, axis=1)[..., None]
    return vals.transpose(0, 1, 3, 2).reshape(g * 512, n)


D, T, I, Q, E, U, Z, C = 512, 2048, 512, 512, 512, 1024, 1024, 256


def setup_inputs():
    n = np.random.standard_normal
    idx = np.random.permutation(T)[:I]
    idx2 = np.random.permutation(U)[:I]
    idx3 = np.random.permutation(Z)[:I]
    idx4 = np.random.permutation(Q)[:C]
    fd = mx_kscale(D)
    fi = mx_kscale(I)
    ti = np.ones(T)
    ti[idx] = fi
    keysp = pack_weight(n((D, T)) / fd[:, None], "e4m3")
    return {
        "query": (n((D, Q)) * 0.6 / np.sqrt(D) * fd[:, None]).astype(np.float32),
        "query2": (n((D, Q)) * 0.6 / np.sqrt(D) * fd[:, None]).astype(np.float32),
        "query3": (n((D, Q)) * 0.6 / np.sqrt(D) * fd[:, None]).astype(np.float32),
        "keys_words": keysp[0],
        "keys_scales": keysp[1],
        "notes": (n((D, U)) / fd[:, None]).astype(np.float32),
        "pages": (n((D, Z)) / fd[:, None]).astype(np.float32),
        "os": (np.random.uniform(0.02, 0.08, (1, I)) * fi).astype(np.float32),
        "vals": (n((E, T)) / ti).astype(np.float32),
        "pgain": (np.random.uniform(0.5, 2.0, (1, C))).astype(np.float32),
        "offs": striped(idx),
        "offs2": striped(idx2),
        "offs3": striped(idx3),
        "offs4": striped(idx4),
    }


def reference(query, query2, query3, keys_words, keys_scales, notes, pages, os, vals, pgain, offs, offs2, offs3, offs4):
    idx = unstriped(offs)
    idx2 = unstriped(offs2)
    idx3 = unstriped(offs3)
    idx4 = unstriped(offs4)
    keysu = unpack_weight(keys_words, keys_scales, "e4m3")
    queryq = mxq(f64(query), 0, "e4m3")
    keysidxg = keysu[:, idx]
    query2q = mxq(f64(query2), 0, "e4m3")
    notesidx2q = mxq(f64(notes)[:, idx2], 0, "e4m3")
    query3q = mxq(f64(query3), 0, "e4m3")
    pagesidx3q = mxq(f64(pages)[:, idx3], 0, "e4m3")
    s = queryq.T @ keysidxg + query2q.T @ notesidx2q + query3q.T @ pagesidx3q
    w = np.maximum(s, 0.0)
    wo1 = w * f64(os)
    wt1 = wo1.T
    vt1 = f64(vals)[:, idx].T
    vt1q = mxq(vt1, 0, "e4m3")
    wt1q = mxq(wt1, 0, "e4m3")
    o = vt1q.T @ wt1q
    y = o[:, idx4] * f64(pgain)
    return y

@@ -1,0 +1,189 @@
+from contextlib import ExitStack
+
+import concourse.mybir as mybir
+from concourse.masks import make_identity
+
+D, T, I, Q, E, U, Z, C = 512, 2048, 512, 512, 512, 1024, 1024, 256
+FLOPS = 2 * 3 * D * I * Q + 2 * I * E * Q
+
+F32 = mybir.dt.float32
+BF16 = mybir.dt.bfloat16
+I32 = mybir.dt.int32
+U32 = mybir.dt.uint32
+U16 = mybir.dt.uint16
+U8 = mybir.dt.uint8
+FP8X4 = mybir.dt.float8_e4m3fn_x4
+COPY = mybir.ActivationFunctionType.Copy
+MAX = mybir.AluOpType.max
+MULT = mybir.AluOpType.mult
+
+P = 128
+PACK = 4
+BLOCKS = 4
+
+
+def tile_attend_threesources_pickedout_lean_kernel(
+    tc, query, query2, query3, keys_words, keys_scales, notes, pages, slot_factors, vals, pgain, offs, offs2, offs3, offs4, out
+):
+    nc = tc.nc
+    with ExitStack() as ctx:
+        keep = ctx.enter_context(tc.tile_pool(name="keep", bufs=1))
+        score_psum = ctx.enter_context(tc.psum_pool(name="score_psum", bufs=1))
+        turn_psum = ctx.enter_context(tc.psum_pool(name="turn_psum", bufs=2))
+        o_psum = ctx.enter_context(tc.psum_pool(name="o_psum", bufs=2))
+
+        def tile(shape, dtype, name):
+            return keep.tile(shape, dtype, name=name, align_bytes=64)
+
+        def load(shape, dtype, name, source):
+            loaded = tile(shape, dtype, name)
+            nc.sync.dma_start(out=loaded[:], in_=source)
+            return loaded
+
+        def load_planes(pool, width, name):
+            planes = pool.rearrange("(p t) u -> t p u", t=PACK)
+            return [load([P, width], F32, "%s_plane%d" % (name, t), planes[t]) for t in range(PACK)]
+
+        def load_query(rows, name):
+            return load([P, PACK, Q], F32, name, rows.rearrange("(p t) q -> p t q", t=PACK))
+
+        identity = tile([P, P], F32, "identity")
+        make_identity(nc, identity[:])
+        key_scale_pool = tile([P, T], U8, "key_scale_pool")
+        nc.vector.memset(key_scale_pool[:].bitcast(I32), 0)
+
+        note_list = load([P, I // 16], U16, "note_list", offs2)
+        note_planes = load_planes(notes, U, "note")
+        page_list = load([P, I // 16], U16, "page_list", offs3)
+        query2_raw = load_query(query2, "query2_raw")
+        token_list = load([P, I // 16], U16, "token_list", offs)
+        page_planes = load_planes(pages, Z, "page")
+        for quadrant in range(4):
+            nc.sync.dma_start(
+                out=key_scale_pool[32 * quadrant : 32 * quadrant + 4, :].bitcast(I32),
+                in_=keys_scales[0, 4 * quadrant : 4 * quadrant + 4, :].bitcast(I32),
+            )
+        query3_raw = load_query(query3, "query3_raw")
+        gain_pairs = load([P, 2], F32, "gain_pairs", pgain.rearrange("o (p j) -> p (o j)", j=2))
+        query_raw = load_query(query, "query_raw")
+        slot_factor = load([P, 1, PACK], F32, "slot_factor", slot_factors.rearrange("o (s r) -> s o r", r=PACK))
+        key_word_pool = tile([P, T], U32, "key_word_pool")
+        nc.sync.dma_start(
+            out=key_word_pool[:].bitcast(I32), in_=keys_words[0].rearrange("p n t -> p (n t)").bitcast(I32)
+        )
+        column_list = load([P, C // 16], U16, "column_list", offs4)
+        value_rows = [load([P, T], F32, "value_rows%d" % j, vals[P * j : P * (j + 1), :]) for j in range(BLOCKS)]
+
+        def quantise(grouped, codes, scales):
+            nc.vector.quantize_mx(out=codes.bitcast(FP8X4), scales=scales, in_=grouped)
+
+        def mx_tiles(width, name):
+            return tile([P, width], U32, name + "_codes"), tile([P, width], U8, name + "_scales")
+
+        def gathered_operand(planes, slots, name):
+            picked = tile([P, PACK, I], BF16, name + "_picked")
+            for t in range(PACK - 1):
+                nc.scalar.activation(picked[:, t, :], planes[t][:].indirect(slots[:]), COPY)
+            nc.vector.tensor_copy(picked[:, PACK - 1, :], planes[PACK - 1][:].indirect(slots[:]))
+            grouped = tile([P, I * PACK], BF16, name + "_grouped")
+            nc.vector.tensor_copy(
+                grouped[:].rearrange("p (r s t) -> p r s t", r=PACK, t=PACK),
+                picked[:].rearrange("p t (s r) -> p r s t", r=PACK),
+            )
+            codes, scales = mx_tiles(I, name)
+            quantise(grouped[:], codes[:], scales[:])
+            return codes, scales
+
+        def query_operand(raw, name):
+            grouped = tile([P, Q * PACK], BF16, name + "_grouped")
+            nc.vector.tensor_copy(
+                grouped[:].rearrange("p (c i t) -> p c t i", i=4, t=PACK),
+                raw[:].rearrange("p t (c i) -> p c t i", i=4),
+            )
+            codes, scales = mx_tiles(Q, name)
+            quantise(grouped[:], codes[:], scales[:])
+            return codes, scales
+
+        banks = [score_psum.tile([P, PACK, P], F32, name="scores%d" % b) for b in range(BLOCKS)]
+
+        def score_passes(picked, queries, first, last):
+            for b in range(BLOCKS):
+                columns = slice(P * b, P * (b + 1))
+                for r in range(PACK):
+                    slots = slice(P * r, P * (r + 1))
+                    nc.tensor.matmul_mx(
+                        out=banks[b][:, r, :],
+                        lhsT=picked[0][:, slots].bitcast(FP8X4),
+                        lhsT_scale=picked[1][:, slots],
+                        rhs=queries[0][:, columns].bitcast(FP8X4),
+                        rhs_scale=queries[1][:, columns],
+                        start=first and r == 0,
+                        stop=last and r == PACK - 1,
+                    )
+
+        gain_bank = turn_psum.tile([P, 2, P], F32, name="turned")
+        for j in range(2):
+            nc.tensor.transpose(gain_bank[:, j, :], gain_pairs[:, j : j + 1].to_broadcast([P, P]), identity[:])
+        gains = tile([P, C], F32, "gains")
+        nc.scalar.copy(gains[:].rearrange("m (p j) -> m p j", j=2), gain_bank[:].rearrange("m j p -> m p j"))
+
+        note_operand = gathered_operand(note_planes, note_list, "note")
+        query2_operand = query_operand(query2_raw, "query2")
+        score_passes(note_operand, query2_operand, True, False)
+
+        key_codes, key_scales = mx_tiles(I, "key")
+        nc.vector.tensor_copy(
+            key_scales[:].rearrange("p (r s) -> p s r", r=PACK), key_scale_pool[:].indirect(token_list[:])
+        )
+        page_operand = gathered_operand(page_planes, page_list, "page")
+        query3_operand = query_operand(query3_raw, "query3")
+        score_passes(page_operand, query3_operand, False, False)
+
+        query_operand1 = query_operand(query_raw, "query")
+        nc.vector.tensor_copy(
+            key_codes[:].rearrange("p (r s) -> p s r", r=PACK), key_word_pool[:].indirect(token_list[:])
+        )
+        score_passes((key_codes, key_scales), query_operand1, False, True)
+
+        weight_codes, weight_scales = mx_tiles(Q, "weight")
+        for b in range(BLOCKS):
+            columns = slice(P * b, P * (b + 1))
+            weights = tile([P, P, PACK], BF16, "weights%d" % b)
+            nc.vector.scalar_tensor_tensor(
+                out=weights[:],
+                in0=banks[b][:].rearrange("s r q -> s q r"),
+                scalar=0.0,
+                in1=slot_factor[:].to_broadcast([P, P, PACK]),
+                op0=MAX,
+                op1=MULT,
+            )
+            quantise(weights[:].rearrange("s q r -> s (q r)"), weight_codes[:, columns], weight_scales[:, columns])
+
+        for j in range(BLOCKS):
+            picked = tile([P, I], BF16, "value_picked%d" % j)
+            nc.scalar.activation(picked[:], value_rows[j][:].indirect(token_list[:]), COPY)
+            pairs = picked[:].bitcast(F32)
+            turned = turn_psum.tile([P, 2, P], F32, name="turned")
+            for u in range(2):
+                nc.tensor.transpose(turned[:, u, :], pairs[:, u : I // 2 : 2], identity[:])
+            grouped = tile([P, P * PACK], BF16, "value_grouped%d" % j)
+            nc.scalar.copy(
+                grouped[:].bitcast(F32).rearrange("s (e u) -> s e u", u=2), turned[:].rearrange("s u e -> s e u")
+            )
+            value_codes, value_scales = mx_tiles(P, "value%d" % j)
+            quantise(grouped[:], value_codes[:], value_scales[:])
+            sums = o_psum.tile([P, Q], F32, name="sums")
+            nc.tensor.matmul_mx(
+                out=sums[:],
+                lhsT=value_codes[:].bitcast(FP8X4),
+                lhsT_scale=value_scales[:],
+                rhs=weight_codes[:].bitcast(FP8X4),
+                rhs_scale=weight_scales[:],
+                start=True,
+                stop=True,
+            )
+            o_rows = tile([P, Q], F32, "o_rows%d" % j)
+            nc.scalar.copy(o_rows[:], sums[:])
+            result = tile([P, C], F32, "result%d" % j)
+            nc.vector.tensor_tensor(result[:], o_rows[:].indirect(column_list[:]), gains[:], MULT)
+            nc.sync.dma_start(out=out[P * j : P * (j + 1), :], in_=result[:])

@@ -20,6 +20,7 @@ MULT = mybir.AluOpType.mult
 P = 128
 PACK = 4
 BLOCKS = 4
+VECTOR_RUNS = 64
 
 
 def tile_attend_threesources_pickedout_lean_kernel(
@@ -28,21 +29,24 @@ def tile_attend_threesources_pickedout_lean_kernel(
     nc = tc.nc
     with ExitStack() as ctx:
         keep = ctx.enter_context(tc.tile_pool(name="keep", bufs=1))
-        score_psum = ctx.enter_context(tc.psum_pool(name="score_psum", bufs=1))
-        turn_psum = ctx.enter_context(tc.psum_pool(name="turn_psum", bufs=2))
-        o_psum = ctx.enter_context(tc.psum_pool(name="o_psum", bufs=2))
+        psum = ctx.enter_context(tc.psum_pool(name="psum", bufs=1))
 
         def tile(shape, dtype, name):
             return keep.tile(shape, dtype, name=name, align_bytes=64)
 
         def load(shape, dtype, name, source):
-            loaded = tile(shape, dtype, name)
+            loaded = keep.tile(shape, dtype, name=name, tag=name, align_bytes=64)
             nc.sync.dma_start(out=loaded[:], in_=source)
             return loaded
 
-        def load_planes(pool, width, name):
-            planes = pool.rearrange("(p t) u -> t p u", t=PACK)
-            return [load([P, width], F32, "%s_plane%d" % (name, t), planes[t]) for t in range(PACK)]
+        def load_plane(pool, width, t, name):
+            return load([P, width], F32, "%s_plane%d" % (name, t), pool.rearrange("(p t) u -> t p u", t=PACK)[t])
+
+        def load_key_scales(quadrant):
+            nc.sync.dma_start(
+                out=key_scale_pool[32 * quadrant : 32 * quadrant + 4, :].bitcast(I32),
+                in_=keys_scales[0, 4 * quadrant : 4 * quadrant + 4, :].bitcast(I32),
+            )
 
         def load_query(rows, name):
             return load([P, PACK, Q], F32, name, rows.rearrange("(p t) q -> p t q", t=PACK))
@@ -53,24 +57,24 @@ def tile_attend_threesources_pickedout_lean_kernel(
         nc.vector.memset(key_scale_pool[:].bitcast(I32), 0)
 
         note_list = load([P, I // 16], U16, "note_list", offs2)
-        note_planes = load_planes(notes, U, "note")
-        page_list = load([P, I // 16], U16, "page_list", offs3)
-        query2_raw = load_query(query2, "query2_raw")
+        note_planes = [load_plane(notes, U, 0, "note")]
         token_list = load([P, I // 16], U16, "token_list", offs)
-        page_planes = load_planes(pages, Z, "page")
-        for quadrant in range(4):
-            nc.sync.dma_start(
-                out=key_scale_pool[32 * quadrant : 32 * quadrant + 4, :].bitcast(I32),
-                in_=keys_scales[0, 4 * quadrant : 4 * quadrant + 4, :].bitcast(I32),
-            )
-        query3_raw = load_query(query3, "query3_raw")
+        note_planes.append(load_plane(notes, U, 1, "note"))
+        page_list = load([P, I // 16], U16, "page_list", offs3)
+        note_planes.append(load_plane(notes, U, 2, "note"))
         gain_pairs = load([P, 2], F32, "gain_pairs", pgain.rearrange("o (p j) -> p (o j)", j=2))
-        query_raw = load_query(query, "query_raw")
-        slot_factor = load([P, 1, PACK], F32, "slot_factor", slot_factors.rearrange("o (s r) -> s o r", r=PACK))
+        note_planes.append(load_plane(notes, U, 3, "note"))
+        for quadrant in range(4):
+            load_key_scales(quadrant)
+        page_planes = [load_plane(pages, Z, t, "page") for t in range(PACK)]
+        query2_raw = load_query(query2, "query2_raw")
+        query3_raw = load_query(query3, "query3_raw")
         key_word_pool = tile([P, T], U32, "key_word_pool")
         nc.sync.dma_start(
             out=key_word_pool[:].bitcast(I32), in_=keys_words[0].rearrange("p n t -> p (n t)").bitcast(I32)
         )
+        slot_factor = load([P, 1, PACK], F32, "slot_factor", slot_factors.rearrange("o (s r) -> s o r", r=PACK))
+        query_raw = load_query(query, "query_raw")
         column_list = load([P, C // 16], U16, "column_list", offs4)
         value_rows = [load([P, T], F32, "value_rows%d" % j, vals[P * j : P * (j + 1), :]) for j in range(BLOCKS)]
 
@@ -80,11 +84,13 @@ def tile_attend_threesources_pickedout_lean_kernel(
         def mx_tiles(width, name):
             return tile([P, width], U32, name + "_codes"), tile([P, width], U8, name + "_scales")
 
-        def gathered_operand(planes, slots, name):
+        def gathered_operand(planes, slots, vector_planes, name):
             picked = tile([P, PACK, I], BF16, name + "_picked")
-            for t in range(PACK - 1):
-                nc.scalar.activation(picked[:, t, :], planes[t][:].indirect(slots[:]), COPY)
-            nc.vector.tensor_copy(picked[:, PACK - 1, :], planes[PACK - 1][:].indirect(slots[:]))
+            for t in range(PACK):
+                if t in vector_planes:
+                    nc.vector.tensor_copy(picked[:, t, :], planes[t][:].indirect(slots[:]))
+                else:
+                    nc.scalar.activation(picked[:, t, :], planes[t][:].indirect(slots[:]), COPY)
             grouped = tile([P, I * PACK], BF16, name + "_grouped")
             nc.vector.tensor_copy(
                 grouped[:].rearrange("p (r s t) -> p r s t", r=PACK, t=PACK),
@@ -96,15 +102,15 @@ def tile_attend_threesources_pickedout_lean_kernel(
 
         def query_operand(raw, name):
             grouped = tile([P, Q * PACK], BF16, name + "_grouped")
-            nc.vector.tensor_copy(
-                grouped[:].rearrange("p (c i t) -> p c t i", i=4, t=PACK),
-                raw[:].rearrange("p t (c i) -> p c t i", i=4),
-            )
+            into = grouped[:].rearrange("p (c i t) -> p c t i", i=4, t=PACK)
+            source = raw[:].rearrange("p t (c i) -> p c t i", i=4)
+            nc.vector.tensor_copy(into[:, :VECTOR_RUNS], source[:, :VECTOR_RUNS])
+            nc.scalar.copy(into[:, VECTOR_RUNS:], source[:, VECTOR_RUNS:])
             codes, scales = mx_tiles(Q, name)
             quantise(grouped[:], codes[:], scales[:])
             return codes, scales
 
-        banks = [score_psum.tile([P, PACK, P], F32, name="scores%d" % b) for b in range(BLOCKS)]
+        banks = [psum.tile([P, PACK, P], F32, name="scores%d" % b, tag="bank%d" % b) for b in range(BLOCKS)]
 
         def score_passes(picked, queries, first, last):
             for b in range(BLOCKS):
@@ -121,69 +127,92 @@ def tile_attend_threesources_pickedout_lean_kernel(
                         stop=last and r == PACK - 1,
                     )
 
-        gain_bank = turn_psum.tile([P, 2, P], F32, name="turned")
+        gain_bank = psum.tile([P, 2, P], F32, name="gain_bank", tag="bank7")
         for j in range(2):
             nc.tensor.transpose(gain_bank[:, j, :], gain_pairs[:, j : j + 1].to_broadcast([P, P]), identity[:])
         gains = tile([P, C], F32, "gains")
         nc.scalar.copy(gains[:].rearrange("m (p j) -> m p j", j=2), gain_bank[:].rearrange("m j p -> m p j"))
 
-        note_operand = gathered_operand(note_planes, note_list, "note")
-        query2_operand = query_operand(query2_raw, "query2")
-        score_passes(note_operand, query2_operand, True, False)
-
         key_codes, key_scales = mx_tiles(I, "key")
         nc.vector.tensor_copy(
             key_scales[:].rearrange("p (r s) -> p s r", r=PACK), key_scale_pool[:].indirect(token_list[:])
         )
-        page_operand = gathered_operand(page_planes, page_list, "page")
-        query3_operand = query_operand(query3_raw, "query3")
-        score_passes(page_operand, query3_operand, False, False)
-
-        query_operand1 = query_operand(query_raw, "query")
+        note_operand = gathered_operand(note_planes, note_list, (1, 3), "note")
+        page_operand = gathered_operand(page_planes, page_list, (3,), "page")
+        score_passes(note_operand, query_operand(query2_raw, "query2"), True, False)
+        score_passes(page_operand, query_operand(query3_raw, "query3"), False, False)
         nc.vector.tensor_copy(
             key_codes[:].rearrange("p (r s) -> p s r", r=PACK), key_word_pool[:].indirect(token_list[:])
         )
-        score_passes((key_codes, key_scales), query_operand1, False, True)
+
+        query_codes, query_scales = mx_tiles(Q, "query")
+        for half, copy in enumerate((nc.vector.tensor_copy, nc.scalar.copy)):
+            columns = slice(half * Q // 2, (half + 1) * Q // 2)
+            grouped = tile([P, Q // 2 * PACK], BF16, "query_grouped%d" % half)
+            copy(
+                grouped[:].rearrange("p (c i t) -> p c t i", i=4, t=PACK),
+                query_raw[:, :, columns].rearrange("p t (c i) -> p c t i", i=4),
+            )
+            quantise(grouped[:], query_codes[:, columns], query_scales[:, columns])
+        score_passes((key_codes, key_scales), (query_codes, query_scales), False, True)
 
         weight_codes, weight_scales = mx_tiles(Q, "weight")
-        for b in range(BLOCKS):
-            columns = slice(P * b, P * (b + 1))
-            weights = tile([P, P, PACK], BF16, "weights%d" % b)
-            nc.vector.scalar_tensor_tensor(
-                out=weights[:],
-                in0=banks[b][:].rearrange("s r q -> s q r"),
-                scalar=0.0,
-                in1=slot_factor[:].to_broadcast([P, P, PACK]),
-                op0=MAX,
-                op1=MULT,
-            )
-            quantise(weights[:].rearrange("s q r -> s (q r)"), weight_codes[:, columns], weight_scales[:, columns])
+        for half in range(2):
+            columns = slice(half * Q // 2, (half + 1) * Q // 2)
+            weights = tile([P, 2, P, PACK], BF16, "weights%d" % half)
+            for b in range(2):
+                nc.vector.scalar_tensor_tensor(
+                    out=weights[:, b],
+                    in0=banks[2 * half + b][:].rearrange("s r q -> s q r"),
+                    scalar=0.0,
+                    in1=slot_factor[:].to_broadcast([P, P, PACK]),
+                    op0=MAX,
+                    op1=MULT,
+                )
+            quantise(weights[:].rearrange("s b q r -> s (b q r)"), weight_codes[:, columns], weight_scales[:, columns])
 
-        for j in range(BLOCKS):
+        def value_operand(j):
             picked = tile([P, I], BF16, "value_picked%d" % j)
-            nc.scalar.activation(picked[:], value_rows[j][:].indirect(token_list[:]), COPY)
+            if j < BLOCKS - 1:
+                nc.scalar.activation(picked[:], value_rows[j][:].indirect(token_list[:]), COPY)
+            else:
+                nc.scalar.activation(picked[:, : I // 2], value_rows[j][:].indirect(token_list[:, : I // 32]), COPY)
+                nc.vector.tensor_copy(picked[:, I // 2 :], value_rows[j][:].indirect(token_list[:, I // 32 :]))
             pairs = picked[:].bitcast(F32)
-            turned = turn_psum.tile([P, 2, P], F32, name="turned")
+            turned = psum.tile([P, 2, P], F32, name="turned%d" % j, tag="bank%d" % (4 + j))
             for u in range(2):
                 nc.tensor.transpose(turned[:, u, :], pairs[:, u : I // 2 : 2], identity[:])
-            grouped = tile([P, P * PACK], BF16, "value_grouped%d" % j)
-            nc.scalar.copy(
+            grouped = keep.tile([P, P * PACK], BF16, name="value_grouped%d" % j, tag="stage%d" % j, align_bytes=64)
+            nc.vector.tensor_copy(
                 grouped[:].bitcast(F32).rearrange("s (e u) -> s e u", u=2), turned[:].rearrange("s u e -> s e u")
             )
-            value_codes, value_scales = mx_tiles(P, "value%d" % j)
-            quantise(grouped[:], value_codes[:], value_scales[:])
-            sums = o_psum.tile([P, Q], F32, name="sums")
+            codes, scales = mx_tiles(P, "value%d" % j)
+            quantise(grouped[:], codes[:], scales[:])
+            return codes, scales
+
+        def output_rows(j, values):
+            sums = psum.tile([P, Q], F32, name="sums%d" % j, tag="bank%d" % j)
             nc.tensor.matmul_mx(
                 out=sums[:],
-                lhsT=value_codes[:].bitcast(FP8X4),
-                lhsT_scale=value_scales[:],
+                lhsT=values[0][:].bitcast(FP8X4),
+                lhsT_scale=values[1][:],
                 rhs=weight_codes[:].bitcast(FP8X4),
                 rhs_scale=weight_scales[:],
                 start=True,
                 stop=True,
             )
-            o_rows = tile([P, Q], F32, "o_rows%d" % j)
-            nc.scalar.copy(o_rows[:], sums[:])
-            result = tile([P, C], F32, "result%d" % j)
+            o_tag = "value_rows%d" % (BLOCKS - 1) if j == 1 else "o_rows%d" % j
+            o_rows = keep.tile([P, Q], F32, name="o_rows%d" % j, tag=o_tag, align_bytes=64)
+            if j == 0:
+                nc.vector.tensor_copy(o_rows[:], sums[:])
+            else:
+                nc.scalar.copy(o_rows[:], sums[:])
+            result = keep.tile([P, C], F32, name="result%d" % j, tag=("stage1", "stage3", "result2", "result3")[j], align_bytes=64)
             nc.vector.tensor_tensor(result[:], o_rows[:].indirect(column_list[:]), gains[:], MULT)
             nc.sync.dma_start(out=out[P * j : P * (j + 1), :], in_=result[:])
+
+        value_operands = [value_operand(0), value_operand(1)]
+        output_rows(0, value_operands[0])
+        value_operands.extend(value_operand(j) for j in range(2, BLOCKS))
+        for j in range(1, BLOCKS):
+            output_rows(j, value_operands[j])

@@ -29,6 +29,7 @@ def tile_attend_threesources_pickedout_lean_kernel(
     nc = tc.nc
     with ExitStack() as ctx:
         keep = ctx.enter_context(tc.tile_pool(name="keep", bufs=1))
+        last = ctx.enter_context(tc.tile_pool(name="last", bufs=1))
         psum = ctx.enter_context(tc.psum_pool(name="psum", bufs=1))
 
         def tile(shape, dtype, name):
@@ -76,7 +77,9 @@ def tile_attend_threesources_pickedout_lean_kernel(
         slot_factor = load([P, 1, PACK], F32, "slot_factor", slot_factors.rearrange("o (s r) -> s o r", r=PACK))
         query_raw = load_query(query, "query_raw")
         column_list = load([P, C // 16], U16, "column_list", offs4)
-        value_rows = [load([P, T], F32, "value_rows%d" % j, vals[P * j : P * (j + 1), :]) for j in range(BLOCKS)]
+        value_rows = [load([P, T], F32, "value_rows%d" % j, vals[P * j : P * (j + 1), :]) for j in range(BLOCKS - 1)]
+        value_rows.append(last.tile([P, T], F32, name="value_rows3", offset=0, align_bytes=64))
+        nc.sync.dma_start(out=value_rows[3][:], in_=vals[P * 3 :, :])
 
         def quantise(grouped, codes, scales):
             nc.vector.quantize_mx(out=codes.bitcast(FP8X4), scales=scales, in_=grouped)
@@ -171,26 +174,37 @@ def tile_attend_threesources_pickedout_lean_kernel(
                 )
             quantise(weights[:].rearrange("s b q r -> s (b q r)"), weight_codes[:, columns], weight_scales[:, columns])
 
-        def value_operand(j):
-            picked = tile([P, I], BF16, "value_picked%d" % j)
+        def pick_values(j):
+            picked = keep.tile([P, I], BF16, name="value_picked%d" % j, tag="value_picked%d" % j, align_bytes=64)
             if j < BLOCKS - 1:
                 nc.scalar.activation(picked[:], value_rows[j][:].indirect(token_list[:]), COPY)
             else:
                 nc.scalar.activation(picked[:, : I // 2], value_rows[j][:].indirect(token_list[:, : I // 32]), COPY)
                 nc.vector.tensor_copy(picked[:, I // 2 :], value_rows[j][:].indirect(token_list[:, I // 32 :]))
+            return picked
+
+        def turn_values(j, picked):
             pairs = picked[:].bitcast(F32)
             turned = psum.tile([P, 2, P], F32, name="turned%d" % j, tag="bank%d" % (4 + j))
             for u in range(2):
                 nc.tensor.transpose(turned[:, u, :], pairs[:, u : I // 2 : 2], identity[:])
-            grouped = keep.tile([P, P * PACK], BF16, name="value_grouped%d" % j, tag="stage%d" % j, align_bytes=64)
+            return turned
+
+        def group_values(turned, grouped):
             nc.vector.tensor_copy(
                 grouped[:].bitcast(F32).rearrange("s (e u) -> s e u", u=2), turned[:].rearrange("s u e -> s e u")
             )
-            codes, scales = mx_tiles(P, "value%d" % j)
+
+        def staging(name, shape, dtype, tag):
+            return keep.tile(shape, dtype, name=name, tag=tag, align_bytes=64)
+
+        def quantise_values(j, grouped, codes_tag):
+            codes = staging("value_codes%d" % j, [P, P], U32, codes_tag)
+            scales = tile([P, P], U8, "value_scales%d" % j)
             quantise(grouped[:], codes[:], scales[:])
             return codes, scales
 
-        def output_rows(j, values):
+        def output_rows(j, values, o_rows, copy, result_tag):
             sums = psum.tile([P, Q], F32, name="sums%d" % j, tag="bank%d" % j)
             nc.tensor.matmul_mx(
                 out=sums[:],
@@ -201,18 +215,28 @@ def tile_attend_threesources_pickedout_lean_kernel(
                 start=True,
                 stop=True,
             )
-            o_tag = "value_rows%d" % (BLOCKS - 1) if j == 1 else "o_rows%d" % j
-            o_rows = keep.tile([P, Q], F32, name="o_rows%d" % j, tag=o_tag, align_bytes=64)
-            if j == 0:
-                nc.vector.tensor_copy(o_rows[:], sums[:])
-            else:
-                nc.scalar.copy(o_rows[:], sums[:])
-            result = keep.tile([P, C], F32, name="result%d" % j, tag=("stage1", "stage3", "result2", "result3")[j], align_bytes=64)
+            copy(o_rows[:], sums[:])
+            result = staging("result%d" % j, [P, C], F32, result_tag)
             nc.vector.tensor_tensor(result[:], o_rows[:].indirect(column_list[:]), gains[:], MULT)
             nc.sync.dma_start(out=out[P * j : P * (j + 1), :], in_=result[:])
 
-        value_operands = [value_operand(0), value_operand(1)]
-        output_rows(0, value_operands[0])
-        value_operands.extend(value_operand(j) for j in range(2, BLOCKS))
-        for j in range(1, BLOCKS):
-            output_rows(j, value_operands[j])
+        values = []
+        for j in range(2):
+            grouped = staging("value_grouped%d" % j, [P, P * PACK], BF16, "value_grouped%d" % j)
+            group_values(turn_values(j, pick_values(j)), grouped)
+            values.append(quantise_values(j, grouped, "value_codes%d" % j))
+        output_rows(0, values[0], tile([P, Q], F32, "o_rows0"), nc.vector.tensor_copy, "value_grouped1")
+
+        turned2 = turn_values(2, pick_values(2))
+        picked3 = pick_values(3)
+        grouped2 = last.tile([P, P * PACK], BF16, name="value_grouped2", offset=Q * 4, align_bytes=64)
+        group_values(turned2, grouped2)
+        turned3 = turn_values(3, picked3)
+        values.append(quantise_values(2, grouped2, "value_picked3"))
+        grouped3 = staging("value_grouped3", [P, P * PACK], BF16, "value_grouped3")
+        group_values(turned3, grouped3)
+        values.append(quantise_values(3, grouped3, "value_codes3"))
+        o_rows1 = last.tile([P, Q], F32, name="o_rows1", offset=0, align_bytes=64)
+        output_rows(1, values[1], o_rows1, nc.scalar.copy, "value_grouped3")
+        for j in (2, 3):
+            output_rows(j, values[j], tile([P, Q], F32, "o_rows%d" % j), nc.scalar.copy, "result%d" % j)

@@ -65,9 +65,10 @@ def tile_attend_threesources_pickedout_lean_kernel(
         note_planes.append(load_plane(notes, U, 2, "note"))
         gain_pairs = load([P, 2], F32, "gain_pairs", pgain.rearrange("o (p j) -> p (o j)", j=2))
         note_planes.append(load_plane(notes, U, 3, "note"))
-        for quadrant in range(4):
-            load_key_scales(quadrant)
-        page_planes = [load_plane(pages, Z, t, "page") for t in range(PACK)]
+        page_planes = []
+        for t in range(PACK):
+            load_key_scales(t)
+            page_planes.append(load_plane(pages, Z, t, "page"))
         query2_raw = load_query(query2, "query2_raw")
         query3_raw = load_query(query3, "query3_raw")
         key_word_pool = tile([P, T], U32, "key_word_pool")
@@ -96,8 +97,8 @@ def tile_attend_threesources_pickedout_lean_kernel(
                     nc.scalar.activation(picked[:, t, :], planes[t][:].indirect(slots[:]), COPY)
             grouped = tile([P, I * PACK], BF16, name + "_grouped")
             nc.vector.tensor_copy(
-                grouped[:].rearrange("p (r s t) -> p r s t", r=PACK, t=PACK),
-                picked[:].rearrange("p t (s r) -> p r s t", r=PACK),
+                grouped[:].rearrange("p (a b s t) -> p a s t b", a=2, b=2, t=PACK),
+                picked[:].rearrange("p t (s a b) -> p a s t b", a=2, b=2),
             )
             codes, scales = mx_tiles(I, name)
             quantise(grouped[:], codes[:], scales[:])
@@ -204,18 +205,21 @@ def tile_attend_threesources_pickedout_lean_kernel(
             quantise(grouped[:], codes[:], scales[:])
             return codes, scales
 
-        def output_rows(j, values, o_rows, copy, result_tag):
-            sums = psum.tile([P, Q], F32, name="sums%d" % j, tag="bank%d" % j)
-            nc.tensor.matmul_mx(
-                out=sums[:],
-                lhsT=values[0][:].bitcast(FP8X4),
-                lhsT_scale=values[1][:],
-                rhs=weight_codes[:].bitcast(FP8X4),
-                rhs_scale=weight_scales[:],
-                start=True,
-                stop=True,
-            )
-            copy(o_rows[:], sums[:])
+        def output_rows(j, values, bank_numbers, o_rows, copy, result_tag):
+            width = Q // len(bank_numbers)
+            for part, bank in enumerate(bank_numbers):
+                columns = slice(width * part, width * (part + 1))
+                sums = psum.tile([P, width], F32, name="sums%d_%d" % (j, part), tag="bank%d" % bank)
+                nc.tensor.matmul_mx(
+                    out=sums[:],
+                    lhsT=values[0][:].bitcast(FP8X4),
+                    lhsT_scale=values[1][:],
+                    rhs=weight_codes[:, columns].bitcast(FP8X4),
+                    rhs_scale=weight_scales[:, columns],
+                    start=True,
+                    stop=True,
+                )
+                copy(o_rows[:, columns], sums[:])
             result = staging("result%d" % j, [P, C], F32, result_tag)
             nc.vector.tensor_tensor(result[:], o_rows[:].indirect(column_list[:]), gains[:], MULT)
             nc.sync.dma_start(out=out[P * j : P * (j + 1), :], in_=result[:])
@@ -225,7 +229,7 @@ def tile_attend_threesources_pickedout_lean_kernel(
             grouped = staging("value_grouped%d" % j, [P, P * PACK], BF16, "value_grouped%d" % j)
             group_values(turn_values(j, pick_values(j)), grouped)
             values.append(quantise_values(j, grouped, "value_codes%d" % j))
-        output_rows(0, values[0], tile([P, Q], F32, "o_rows0"), nc.vector.tensor_copy, "value_grouped1")
+        output_rows(0, values[0], (0,), tile([P, Q], F32, "o_rows0"), nc.vector.tensor_copy, "value_grouped1")
 
         turned2 = turn_values(2, pick_values(2))
         picked3 = pick_values(3)
@@ -237,6 +241,6 @@ def tile_attend_threesources_pickedout_lean_kernel(
         group_values(turned3, grouped3)
         values.append(quantise_values(3, grouped3, "value_codes3"))
         o_rows1 = last.tile([P, Q], F32, name="o_rows1", offset=0, align_bytes=64)
-        output_rows(1, values[1], o_rows1, nc.scalar.copy, "value_grouped3")
-        for j in (2, 3):
-            output_rows(j, values[j], tile([P, Q], F32, "o_rows%d" % j), nc.scalar.copy, "result%d" % j)
+        output_rows(1, values[1], (1,), o_rows1, nc.scalar.copy, "value_grouped3")
+        for j, bank_numbers in ((2, (2,)), (3, (3, 0))):
+            output_rows(j, values[j], bank_numbers, tile([P, Q], F32, "o_rows%d" % j), nc.scalar.copy, "result%d" % j)

@@ -57,10 +57,10 @@ def tile_attend_threesources_pickedout_lean_kernel(
         key_scale_pool = tile([P, T], U8, "key_scale_pool")
         nc.vector.memset(key_scale_pool[:].bitcast(I32), 0)
 
-        note_list = load([P, I // 16], U16, "note_list", offs2)
         note_planes = [load_plane(notes, U, 0, "note")]
-        token_list = load([P, I // 16], U16, "token_list", offs)
+        note_list = load([P, I // 16], U16, "note_list", offs2)
         note_planes.append(load_plane(notes, U, 1, "note"))
+        token_list = load([P, I // 16], U16, "token_list", offs)
         page_list = load([P, I // 16], U16, "page_list", offs3)
         note_planes.append(load_plane(notes, U, 2, "note"))
         gain_pairs = load([P, 2], F32, "gain_pairs", pgain.rearrange("o (p j) -> p (o j)", j=2))
@@ -191,23 +191,21 @@ def tile_attend_threesources_pickedout_lean_kernel(
                 nc.tensor.transpose(turned[:, u, :], pairs[:, u : I // 2 : 2], identity[:])
             return turned
 
-        def group_values(turned, grouped):
-            nc.vector.tensor_copy(
-                grouped[:].bitcast(F32).rearrange("s (e u) -> s e u", u=2), turned[:].rearrange("s u e -> s e u")
-            )
+        def group_values(turned, grouped, copy):
+            copy(grouped[:].bitcast(F32).rearrange("s (e u) -> s e u", u=2), turned[:].rearrange("s u e -> s e u"))
+            return grouped
 
         def staging(name, shape, dtype, tag):
             return keep.tile(shape, dtype, name=name, tag=tag, align_bytes=64)
 
-        def quantise_values(j, grouped, codes_tag):
-            codes = staging("value_codes%d" % j, [P, P], U32, codes_tag)
+        def quantise_values(j, grouped, codes):
             scales = tile([P, P], U8, "value_scales%d" % j)
             quantise(grouped[:], codes[:], scales[:])
             return codes, scales
 
-        def output_rows(j, values, bank_numbers, o_rows, copy, result_tag):
-            width = Q // len(bank_numbers)
-            for part, bank in enumerate(bank_numbers):
+        def sum_rows(j, values, parts, o_rows):
+            width = Q // len(parts)
+            for part, (bank, copy) in enumerate(parts):
                 columns = slice(width * part, width * (part + 1))
                 sums = psum.tile([P, width], F32, name="sums%d_%d" % (j, part), tag="bank%d" % bank)
                 nc.tensor.matmul_mx(
@@ -220,27 +218,34 @@ def tile_attend_threesources_pickedout_lean_kernel(
                     stop=True,
                 )
                 copy(o_rows[:, columns], sums[:])
-            result = staging("result%d" % j, [P, C], F32, result_tag)
+            return o_rows
+
+        def give_out(j, o_rows, result):
             nc.vector.tensor_tensor(result[:], o_rows[:].indirect(column_list[:]), gains[:], MULT)
             nc.sync.dma_start(out=out[P * j : P * (j + 1), :], in_=result[:])
 
+        def over_last_rows(name, shape, dtype, offset):
+            return last.tile(shape, dtype, name=name, offset=offset, align_bytes=64)
+
+        on_vector, on_scalar = nc.vector.tensor_copy, nc.scalar.copy
         values = []
         for j in range(2):
             grouped = staging("value_grouped%d" % j, [P, P * PACK], BF16, "value_grouped%d" % j)
-            group_values(turn_values(j, pick_values(j)), grouped)
-            values.append(quantise_values(j, grouped, "value_codes%d" % j))
-        output_rows(0, values[0], (0,), tile([P, Q], F32, "o_rows0"), nc.vector.tensor_copy, "value_grouped1")
+            group_values(turn_values(j, pick_values(j)), grouped, on_vector)
+            values.append(quantise_values(j, grouped, tile([P, P], U32, "value_codes%d" % j)))
+        o_rows0 = sum_rows(0, values[0], ((0, on_vector),), tile([P, Q], F32, "o_rows0"))
+        give_out(0, o_rows0, staging("result0", [P, C], F32, "value_grouped1"))
 
         turned2 = turn_values(2, pick_values(2))
         picked3 = pick_values(3)
-        grouped2 = last.tile([P, P * PACK], BF16, name="value_grouped2", offset=Q * 4, align_bytes=64)
-        group_values(turned2, grouped2)
+        grouped2 = group_values(turned2, over_last_rows("value_grouped2", [P, P * PACK], BF16, Q * 4), on_vector)
         turned3 = turn_values(3, picked3)
-        values.append(quantise_values(2, grouped2, "value_picked3"))
-        grouped3 = staging("value_grouped3", [P, P * PACK], BF16, "value_grouped3")
-        group_values(turned3, grouped3)
-        values.append(quantise_values(3, grouped3, "value_codes3"))
-        o_rows1 = last.tile([P, Q], F32, name="o_rows1", offset=0, align_bytes=64)
-        output_rows(1, values[1], (1,), o_rows1, nc.scalar.copy, "value_grouped3")
-        for j, bank_numbers in ((2, (2,)), (3, (3, 0))):
-            output_rows(j, values[j], bank_numbers, tile([P, Q], F32, "o_rows%d" % j), nc.scalar.copy, "result%d" % j)
+        o_rows1 = sum_rows(1, values[1], ((1, on_scalar),), over_last_rows("o_rows1", [P, Q], F32, 0))
+        grouped3 = group_values(turned3, staging("value_grouped3", [P, P * PACK], BF16, "value_grouped3"), on_scalar)
+        values.append(quantise_values(2, grouped2, staging("value_codes2", [P, P], U32, "value_picked3")))
+        values.append(quantise_values(3, grouped3, tile([P, P], U32, "value_codes3")))
+        give_out(1, o_rows1, staging("result1", [P, C], F32, "value_grouped3"))
+        o_rows2 = sum_rows(2, values[2], ((2, on_scalar),), tile([P, Q], F32, "o_rows2"))
+        give_out(2, o_rows2, tile([P, C], F32, "result2"))
+        o_rows3 = sum_rows(3, values[3], ((3, on_scalar), (0, on_scalar)), tile([P, Q], F32, "o_rows3"))
+        give_out(3, o_rows3, tile([P, C], F32, "result3"))

from contextlib import ExitStack

import concourse.mybir as mybir
from concourse.masks import make_identity

D, T, I, Q, E, U, Z, C = 512, 2048, 512, 512, 512, 1024, 1024, 256
FLOPS = 2 * 3 * D * I * Q + 2 * I * E * Q

F32 = mybir.dt.float32
BF16 = mybir.dt.bfloat16
I32 = mybir.dt.int32
U32 = mybir.dt.uint32
U16 = mybir.dt.uint16
U8 = mybir.dt.uint8
FP8X4 = mybir.dt.float8_e4m3fn_x4
COPY = mybir.ActivationFunctionType.Copy
MAX = mybir.AluOpType.max
MULT = mybir.AluOpType.mult

P = 128
PACK = 4
BLOCKS = 4
VECTOR_RUNS = 64


def tile_attend_threesources_pickedout_lean_kernel(
    tc, query, query2, query3, keys_words, keys_scales, notes, pages, slot_factors, vals, pgain, offs, offs2, offs3, offs4, out
):
    nc = tc.nc
    with ExitStack() as ctx:
        keep = ctx.enter_context(tc.tile_pool(name="keep", bufs=1))
        last = ctx.enter_context(tc.tile_pool(name="last", bufs=1))
        psum = ctx.enter_context(tc.psum_pool(name="psum", bufs=1))

        def tile(shape, dtype, name):
            return keep.tile(shape, dtype, name=name, align_bytes=64)

        def load(shape, dtype, name, source):
            loaded = keep.tile(shape, dtype, name=name, tag=name, align_bytes=64)
            nc.sync.dma_start(out=loaded[:], in_=source)
            return loaded

        def load_plane(pool, width, t, name):
            return load([P, width], F32, "%s_plane%d" % (name, t), pool.rearrange("(p t) u -> t p u", t=PACK)[t])

        def load_key_scales(quadrant):
            nc.sync.dma_start(
                out=key_scale_pool[32 * quadrant : 32 * quadrant + 4, :].bitcast(I32),
                in_=keys_scales[0, 4 * quadrant : 4 * quadrant + 4, :].bitcast(I32),
            )

        def load_query(rows, name):
            return load([P, PACK, Q], F32, name, rows.rearrange("(p t) q -> p t q", t=PACK))

        identity = tile([P, P], F32, "identity")
        make_identity(nc, identity[:])
        key_scale_pool = tile([P, T], U8, "key_scale_pool")
        nc.vector.memset(key_scale_pool[:].bitcast(I32), 0)

        note_planes = [load_plane(notes, U, 0, "note")]
        note_list = load([P, I // 16], U16, "note_list", offs2)
        note_planes.append(load_plane(notes, U, 1, "note"))
        token_list = load([P, I // 16], U16, "token_list", offs)
        page_list = load([P, I // 16], U16, "page_list", offs3)
        note_planes.append(load_plane(notes, U, 2, "note"))
        gain_pairs = load([P, 2], F32, "gain_pairs", pgain.rearrange("o (p j) -> p (o j)", j=2))
        note_planes.append(load_plane(notes, U, 3, "note"))
        page_planes = []
        for t in range(PACK):
            load_key_scales(t)
            page_planes.append(load_plane(pages, Z, t, "page"))
        query2_raw = load_query(query2, "query2_raw")
        query3_raw = load_query(query3, "query3_raw")
        key_word_pool = tile([P, T], U32, "key_word_pool")
        nc.sync.dma_start(
            out=key_word_pool[:].bitcast(I32), in_=keys_words[0].rearrange("p n t -> p (n t)").bitcast(I32)
        )
        slot_factor = load([P, 1, PACK], F32, "slot_factor", slot_factors.rearrange("o (s r) -> s o r", r=PACK))
        query_raw = load_query(query, "query_raw")
        column_list = load([P, C // 16], U16, "column_list", offs4)
        value_rows = [load([P, T], F32, "value_rows%d" % j, vals[P * j : P * (j + 1), :]) for j in range(BLOCKS - 1)]
        value_rows.append(last.tile([P, T], F32, name="value_rows3", offset=0, align_bytes=64))
        nc.sync.dma_start(out=value_rows[3][:], in_=vals[P * 3 :, :])

        def quantise(grouped, codes, scales):
            nc.vector.quantize_mx(out=codes.bitcast(FP8X4), scales=scales, in_=grouped)

        def mx_tiles(width, name):
            return tile([P, width], U32, name + "_codes"), tile([P, width], U8, name + "_scales")

        def gathered_operand(planes, slots, vector_planes, name):
            picked = tile([P, PACK, I], BF16, name + "_picked")
            for t in range(PACK):
                if t in vector_planes:
                    nc.vector.tensor_copy(picked[:, t, :], planes[t][:].indirect(slots[:]))
                else:
                    nc.scalar.activation(picked[:, t, :], planes[t][:].indirect(slots[:]), COPY)
            grouped = tile([P, I * PACK], BF16, name + "_grouped")
            nc.vector.tensor_copy(
                grouped[:].rearrange("p (a b s t) -> p a s t b", a=2, b=2, t=PACK),
                picked[:].rearrange("p t (s a b) -> p a s t b", a=2, b=2),
            )
            codes, scales = mx_tiles(I, name)
            quantise(grouped[:], codes[:], scales[:])
            return codes, scales

        def query_operand(raw, name):
            grouped = tile([P, Q * PACK], BF16, name + "_grouped")
            into = grouped[:].rearrange("p (c i t) -> p c t i", i=4, t=PACK)
            source = raw[:].rearrange("p t (c i) -> p c t i", i=4)
            nc.vector.tensor_copy(into[:, :VECTOR_RUNS], source[:, :VECTOR_RUNS])
            nc.scalar.copy(into[:, VECTOR_RUNS:], source[:, VECTOR_RUNS:])
            codes, scales = mx_tiles(Q, name)
            quantise(grouped[:], codes[:], scales[:])
            return codes, scales

        banks = [psum.tile([P, PACK, P], F32, name="scores%d" % b, tag="bank%d" % b) for b in range(BLOCKS)]

        def score_passes(picked, queries, first, last):
            for b in range(BLOCKS):
                columns = slice(P * b, P * (b + 1))
                for r in range(PACK):
                    slots = slice(P * r, P * (r + 1))
                    nc.tensor.matmul_mx(
                        out=banks[b][:, r, :],
                        lhsT=picked[0][:, slots].bitcast(FP8X4),
                        lhsT_scale=picked[1][:, slots],
                        rhs=queries[0][:, columns].bitcast(FP8X4),
                        rhs_scale=queries[1][:, columns],
                        start=first and r == 0,
                        stop=last and r == PACK - 1,
                    )

        gain_bank = psum.tile([P, 2, P], F32, name="gain_bank", tag="bank7")
        for j in range(2):
            nc.tensor.transpose(gain_bank[:, j, :], gain_pairs[:, j : j + 1].to_broadcast([P, P]), identity[:])
        gains = tile([P, C], F32, "gains")
        nc.scalar.copy(gains[:].rearrange("m (p j) -> m p j", j=2), gain_bank[:].rearrange("m j p -> m p j"))

        key_codes, key_scales = mx_tiles(I, "key")
        nc.vector.tensor_copy(
            key_scales[:].rearrange("p (r s) -> p s r", r=PACK), key_scale_pool[:].indirect(token_list[:])
        )
        note_operand = gathered_operand(note_planes, note_list, (1, 3), "note")
        page_operand = gathered_operand(page_planes, page_list, (3,), "page")
        score_passes(note_operand, query_operand(query2_raw, "query2"), True, False)
        score_passes(page_operand, query_operand(query3_raw, "query3"), False, False)
        nc.vector.tensor_copy(
            key_codes[:].rearrange("p (r s) -> p s r", r=PACK), key_word_pool[:].indirect(token_list[:])
        )

        query_codes, query_scales = mx_tiles(Q, "query")
        for half, copy in enumerate((nc.vector.tensor_copy, nc.scalar.copy)):
            columns = slice(half * Q // 2, (half + 1) * Q // 2)
            grouped = tile([P, Q // 2 * PACK], BF16, "query_grouped%d" % half)
            copy(
                grouped[:].rearrange("p (c i t) -> p c t i", i=4, t=PACK),
                query_raw[:, :, columns].rearrange("p t (c i) -> p c t i", i=4),
            )
            quantise(grouped[:], query_codes[:, columns], query_scales[:, columns])
        score_passes((key_codes, key_scales), (query_codes, query_scales), False, True)

        weight_codes, weight_scales = mx_tiles(Q, "weight")
        for half in range(2):
            columns = slice(half * Q // 2, (half + 1) * Q // 2)
            weights = tile([P, 2, P, PACK], BF16, "weights%d" % half)
            for b in range(2):
                nc.vector.scalar_tensor_tensor(
                    out=weights[:, b],
                    in0=banks[2 * half + b][:].rearrange("s r q -> s q r"),
                    scalar=0.0,
                    in1=slot_factor[:].to_broadcast([P, P, PACK]),
                    op0=MAX,
                    op1=MULT,
                )
            quantise(weights[:].rearrange("s b q r -> s (b q r)"), weight_codes[:, columns], weight_scales[:, columns])

        def pick_values(j):
            picked = keep.tile([P, I], BF16, name="value_picked%d" % j, tag="value_picked%d" % j, align_bytes=64)
            if j < BLOCKS - 1:
                nc.scalar.activation(picked[:], value_rows[j][:].indirect(token_list[:]), COPY)
            else:
                nc.scalar.activation(picked[:, : I // 2], value_rows[j][:].indirect(token_list[:, : I // 32]), COPY)
                nc.vector.tensor_copy(picked[:, I // 2 :], value_rows[j][:].indirect(token_list[:, I // 32 :]))
            return picked

        def turn_values(j, picked):
            pairs = picked[:].bitcast(F32)
            turned = psum.tile([P, 2, P], F32, name="turned%d" % j, tag="bank%d" % (4 + j))
            for u in range(2):
                nc.tensor.transpose(turned[:, u, :], pairs[:, u : I // 2 : 2], identity[:])
            return turned

        def group_values(turned, grouped, copy):
            copy(grouped[:].bitcast(F32).rearrange("s (e u) -> s e u", u=2), turned[:].rearrange("s u e -> s e u"))
            return grouped

        def staging(name, shape, dtype, tag):
            return keep.tile(shape, dtype, name=name, tag=tag, align_bytes=64)

        def quantise_values(j, grouped, codes):
            scales = tile([P, P], U8, "value_scales%d" % j)
            quantise(grouped[:], codes[:], scales[:])
            return codes, scales

        def sum_rows(j, values, parts, o_rows):
            width = Q // len(parts)
            for part, (bank, copy) in enumerate(parts):
                columns = slice(width * part, width * (part + 1))
                sums = psum.tile([P, width], F32, name="sums%d_%d" % (j, part), tag="bank%d" % bank)
                nc.tensor.matmul_mx(
                    out=sums[:],
                    lhsT=values[0][:].bitcast(FP8X4),
                    lhsT_scale=values[1][:],
                    rhs=weight_codes[:, columns].bitcast(FP8X4),
                    rhs_scale=weight_scales[:, columns],
                    start=True,
                    stop=True,
                )
                copy(o_rows[:, columns], sums[:])
            return o_rows

        def give_out(j, o_rows, result):
            nc.vector.tensor_tensor(result[:], o_rows[:].indirect(column_list[:]), gains[:], MULT)
            nc.sync.dma_start(out=out[P * j : P * (j + 1), :], in_=result[:])

        def over_last_rows(name, shape, dtype, offset):
            return last.tile(shape, dtype, name=name, offset=offset, align_bytes=64)

        on_vector, on_scalar = nc.vector.tensor_copy, nc.scalar.copy
        values = []
        for j in range(2):
            grouped = staging("value_grouped%d" % j, [P, P * PACK], BF16, "value_grouped%d" % j)
            group_values(turn_values(j, pick_values(j)), grouped, on_vector)
            values.append(quantise_values(j, grouped, tile([P, P], U32, "value_codes%d" % j)))
        o_rows0 = sum_rows(0, values[0], ((0, on_vector),), tile([P, Q], F32, "o_rows0"))
        give_out(0, o_rows0, staging("result0", [P, C], F32, "value_grouped1"))

        turned2 = turn_values(2, pick_values(2))
        picked3 = pick_values(3)
        grouped2 = group_values(turned2, over_last_rows("value_grouped2", [P, P * PACK], BF16, Q * 4), on_vector)
        turned3 = turn_values(3, picked3)
        o_rows1 = sum_rows(1, values[1], ((1, on_scalar),), over_last_rows("o_rows1", [P, Q], F32, 0))
        grouped3 = group_values(turned3, staging("value_grouped3", [P, P * PACK], BF16, "value_grouped3"), on_scalar)
        values.append(quantise_values(2, grouped2, staging("value_codes2", [P, P], U32, "value_picked3")))
        values.append(quantise_values(3, grouped3, tile([P, P], U32, "value_codes3")))
        give_out(1, o_rows1, staging("result1", [P, C], F32, "value_grouped3"))
        o_rows2 = sum_rows(2, values[2], ((2, on_scalar),), tile([P, Q], F32, "o_rows2"))
        give_out(2, o_rows2, tile([P, C], F32, "result2"))
        o_rows3 = sum_rows(3, values[3], ((3, on_scalar), (0, on_scalar)), tile([P, Q], F32, "o_rows3"))
        give_out(3, o_rows3, tile([P, C], F32, "result3"))
